import numpy as np, ml_dtypes
CORES = [7,15,23,39,47,63,71,79,87,95,119,127]
N = 12
W, KW, DIL = 64, 7, 1
H = (KW // 2) * DIL
def setup_inputs(rng):
    return {"x": rng.standard_normal((N, 128, W), dtype=np.float32).astype(ml_dtypes.bfloat16), "w": rng.standard_normal((N, 128, KW * 128), dtype=np.float32).astype(ml_dtypes.bfloat16)}
def setup_inputs_big(rng):
    d = setup_inputs(rng)
    for k in ("x", "w"): d[k] = (d[k].astype(np.float32) * 1024.0).astype(d[k].dtype)
    return d
def setup_inputs_small(rng):
    d = setup_inputs(rng)
    for k in ("x", "w"): d[k] = (d[k].astype(np.float32) * (1 / 1024.0)).astype(d[k].dtype)
    return d
def reference(x, w):
    X, W_ = x.astype(np.float64), w.astype(np.float64)
    g = np.concatenate(list(X), axis=1)
    p = np.concatenate([g[:, -H:], g, g[:, :H]], axis=1)
    y = np.zeros((N, 128, W))
    for r in range(N):
        for i in range(KW):
            y[r] += W_[r][:, 128 * i:128 * i + 128].T @ p[:, W * r + i * DIL:W * r + i * DIL + W]
    return {"y": y.astype(ml_dtypes.bfloat16 if x.dtype != np.float64 else np.float64)}

from concourse.bass import DstId, RemoteDMATransfer

W = 64
KW = 7
H = KW // 2
C = 128

SCRATCH = {
    "xs": ("sbuf", [C, W], "bfloat16"),
    "ws": ("sbuf", [C, KW * C], "bfloat16"),
    "hl": ("sbuf", [C, H], "bfloat16"),
    "hr": ("sbuf", [C, H], "bfloat16"),
    "acc": ("psum", [C, W], "float32"),
    "ys": ("sbuf", [C, W], "bfloat16"),
}
SEMAPHORES = ["xl", "wl", "sent", "arl", "arr", "mm", "cp", "st"]

ENGINES_EACH = 4


def _links(topo, a, b):
    ca, cb = topo.chip(a), topo.chip(b)
    return 1 if (topo.mates(ca, cb) or topo.same_plane(ca, cb)) else 2


def _bits(mask):
    return [1 << e for e in range(mask.bit_length()) if (mask >> e) & 1]


def rank_program(g, core, T, topo):
    rank = T.rank_of(core)
    if rank is None:
        return
    n = len(T.cores)
    left, right = T.cores[(rank - 1) % n], T.cores[(rank + 1) % n]
    assert topo.may_write(core, left) and topo.may_write(core, right)
    S = T.sem

    g.sync.dma_start(T.xs[:], T.x[:]).then_inc(S.xl, 16)
    g.sync.dma_start(T.ws[:], T.w[:]).then_inc(S.wl, 16)

    eng = _bits(topo.mask(core, left) & topo.mask(core, right))
    ml, mr = sum(eng[:ENGINES_EACH]), sum(eng[ENGINES_EACH:2 * ENGINES_EACH])
    rl, pl, _ = topo.addr(left)
    rr, pr, _ = topo.addr(right)
    g.wait_ge(S.xl, 16)
    g.remote_dma_fused([
        RemoteDMATransfer(dst_ids=[DstId(rid=rl, pnc=pl)], dma_engine_mask=ml, remote_sem=S.arr,
                          src=T.xs[:, 0:H], dst=T.hr[:]),
        RemoteDMATransfer(dst_ids=[DstId(rid=rr, pnc=pr)], dma_engine_mask=mr, remote_sem=S.arl,
                          src=T.xs[:, W - H:W], dst=T.hl[:]),
    ], local_sem=S.sent)

    te = g.tensor
    te.wait_ge(S.xl, 16)
    te.wait_ge(S.wl, 16)

    def tile(i):
        return T.ws[:, C * i:C * (i + 1)]

    te.matmul(T.acc[:], tile(H), T.xs[:], start=True, stop=False)
    for i in range(KW):
        if i == H:
            continue
        lo, hi = max(0, H - i), min(W, W + H - i)
        te.matmul(T.acc[:, lo:hi], tile(i), T.xs[:, lo + i - H:hi + i - H], start=False, stop=False)

    def left_part(last):
        te.wait_ge(S.arl, ENGINES_EACH)
        out = None
        for i in range(H):
            out = te.matmul(T.acc[:, 0:H - i], tile(i), T.hl[:, i:H], start=False, stop=last and i == H - 1)
        return out

    def right_part(last):
        te.wait_ge(S.arr, ENGINES_EACH)
        out = None
        for k in range(1, H + 1):
            out = te.matmul(T.acc[:, W - k:W], tile(H + k), T.hr[:, 0:k], start=False, stop=last and k == H)
        return out

    if _links(topo, left, core) <= _links(topo, right, core):
        left_part(False)
        fin = right_part(True)
    else:
        right_part(False)
        fin = left_part(True)
    fin.then_inc(S.mm, 1)

    g.vector.wait_ge(S.mm, 1)
    g.vector.tensor_copy(T.ys[:], T.acc[:]).then_inc(S.cp, 1)
    g.scalar.wait_ge(S.cp, 1)
    g.scalar.dma_start(T.y[:], T.ys[:]).then_inc(S.st, 16)
    g.scalar.wait_ge(S.st, 16)
    g.wait_ge(S.sent, 2 * ENGINES_EACH)
